import numpy as np
import ml_dtypes


def mxq(x, axis, fmt="e4m3"):
    dtype, down = {"e4m3": (ml_dtypes.float8_e4m3fn, 7), "e5m2": (ml_dtypes.float8_e5m2, 14)}[fmt]
    v = np.moveaxis(np.asarray(x, np.float32).astype(ml_dtypes.bfloat16).astype(np.float64), axis, -1)
    blocks = v.reshape(v.shape[:-1] + (-1, 32))
    amax = np.abs(blocks).max(-1, keepdims=True)
    byte = np.maximum(np.where(amax > 0, np.frexp(amax)[1] - 1 + 127, 0) - down, 1)
    scale = np.exp2(byte - 127.0)
    codes = (blocks / scale).astype(np.float32).astype(dtype).astype(np.float64)
    return np.moveaxis((codes * scale).reshape(v.shape), -1, axis)


WIDE = False


def mx_kscale(k):
    if not WIDE:
        return np.ones(k)
    levels = np.array([10, -10, 5, -5, 0])
    if k % 512:
        return np.exp2(np.random.permutation(np.resize(levels, k // 32))).repeat(32)
    a = np.empty((k // 512, 16))
    for p in range(k // 512):
        a[p, :8] = np.random.permutation(np.resize(levels, 8))
        for g in range(8):
            far = levels[np.abs(levels - a[p, g]) >= 10]
            a[p, g + 8] = far[np.random.randint(len(far))]
    return np.exp2(a.ravel()).repeat(32)


def f64(x):
    return np.asarray(x).astype(np.float64)


def striped(idx):
    return np.tile(idx.reshape(-1, 16).T, (8, 1)).astype(np.uint16)


def unstriped(offs):
    return offs[:16].T.reshape(-1).astype(np.int64)


def pack_weight(w):
    k, n = w.shape
    w = f64(np.asarray(w, np.float32).astype(ml_dtypes.bfloat16)).reshape(k // 32, 32, n)
    amax = np.abs(w).max(1)
    byte = np.clip(np.where(amax > 0, np.frexp(amax)[1] - 1 + 127 - 7, 1), 1, 254)
    scaled = (w * np.exp2(127.0 - byte)[:, None, :]).reshape(k, n).astype(np.float32)
    words = np.ascontiguousarray(scaled.reshape(k // 512, 128, 4, n).transpose(0, 1, 3, 2)).astype(ml_dtypes.float8_e4m3fn).view(np.uint8)
    return words, np.ascontiguousarray(byte.astype(np.uint8).reshape(k // 512, 16, n))


def unpack_weight(words, scales):
    g, p, n, _ = words.shape
    vals = np.ascontiguousarray(words).view(ml_dtypes.float8_e4m3fn).astype(np.float64) * np.repeat(np.exp2(scales.astype(np.float64) - 127.0), 8, axis=1)[..., None]
    return vals.transpose(0, 1, 3, 2).reshape(g * 512, n)


K, T, E, C, N = 512, 512, 8, 128, 512


def by_expert(wq, xq):
    return np.concatenate([wq[e].T @ xq[:, e * C:(e + 1) * C] for e in range(E)], axis=1)


def setup_inputs():
    n = np.random.standard_normal
    s = mx_kscale(K)[:, None]
    first = np.random.permutation(np.repeat(np.arange(E), T // E))
    second = (first + 1 + np.random.permutation(np.repeat(np.arange(E - 1), -(-T // (E - 1)))[:T])) % E
    while np.bincount(second, minlength=E).max() != T // E:
        load = np.bincount(second, minlength=E); hi, lo = int(load.argmax()), int(load.argmin())
        t = np.flatnonzero((second == hi) & (first != lo))[0]; second[t] = lo
    slot_token = np.empty(E * C, np.int64); pos = np.empty((2, T), np.int64); fill = np.zeros(E, np.int64)
    place = np.stack([np.random.permutation(C) for _ in range(E)])
    for r, deal in enumerate((first, second)):
        for t in np.random.permutation(T):
            e = deal[t]; j = e * C + place[e, fill[e]]; fill[e] += 1; slot_token[j] = t; pos[r, t] = j
    g = np.random.uniform(0.2, 0.8, T)
    packed = [pack_weight(m) for m in n((E, K, N)) / np.sqrt(K) / s[None]]
    return {
        "xT": (n((K, T)) * s).astype(np.float32),
        "w_words": np.stack([m[0] for m in packed]),
        "w_scales": np.stack([m[1] for m in packed]),
        "gate": np.stack([np.tile(g, (N, 1)), np.tile(1.0 - g, (N, 1))]).astype(np.float32),
        "offs": striped(slot_token),
        "pos1": striped(pos[0]),
        "pos2": striped(pos[1]),
    }


def reference(xT, w_words, w_scales, gate, offs, pos1, pos2):
    idx = unstriped(offs)
    xq = mxq(f64(xT)[:, idx], 0, "e4m3")
    w = np.stack([unpack_weight(w_words[e], w_scales[e]) for e in range(E)])
    y = by_expert(w, xq)
    return f64(gate[0]) * y[:, unstriped(pos1)] + f64(gate[1]) * y[:, unstriped(pos2)]

@@ -1,0 +1,173 @@
+from contextlib import ExitStack
+
+import concourse.mybir as mybir
+from concourse.masks import make_identity
+
+K, T, E, C, N = 512, 512, 8, 128, 512
+FLOPS = 2 * K * N * E * C
+
+F32 = mybir.dt.float32
+BF16 = mybir.dt.bfloat16
+I32 = mybir.dt.int32
+U32 = mybir.dt.uint32
+U16 = mybir.dt.uint16
+U8 = mybir.dt.uint8
+FP8X4 = mybir.dt.float8_e4m3fn_x4
+MULT = mybir.AluOpType.mult
+ADD = mybir.AluOpType.add
+
+P = 128
+PACK = 4
+SLOTS = E * C
+NB = N // P
+X_CHUNKS = (256, 128, 128)
+GATHERS = (384, 384, 256)
+BANK = 512
+
+
+def tile_routed_moe_kernel(tc, xT, w_words, w_scales, gate, offs, pos1, pos2, out):
+    nc = tc.nc
+    with ExitStack() as ctx:
+        lists = ctx.enter_context(tc.tile_pool(name="lists", bufs=1))
+        keep = ctx.enter_context(tc.tile_pool(name="keep", bufs=1))
+        psum = ctx.enter_context(tc.psum_pool(name="psum", bufs=1))
+
+        offs_t = lists.tile([P, SLOTS // 16], U16, name="offs_t")
+        pos1_t = lists.tile([P, T // 16], U16, name="pos1_t")
+        pos2_t = lists.tile([P, T // 16], U16, name="pos2_t")
+
+        x_view = xT.rearrange("(p j) n -> p j n", j=PACK)
+        x_raw = []
+        t0 = 0
+        for i, cw in enumerate(X_CHUNKS):
+            raw = keep.tile([P, PACK, cw], F32, name="x_raw%d" % i)
+            nc.sync.dma_start(out=raw[:], in_=x_view[:, :, t0 : t0 + cw])
+            x_raw.append((raw, t0, cw))
+            t0 += cw
+        nc.sync.dma_start(offs_t[:], offs)
+
+        ident = keep.tile([P, P], F32, name="ident")
+        make_identity(nc, ident[:])
+
+        x_codes = keep.tile([P, T], U32, name="x_codes", align_bytes=64)
+        x_scales = keep.tile([P, T], U8, name="x_scales", align_bytes=64)
+        nc.gpsimd.memset(x_scales[:], 0)
+
+        w_sc = keep.tile([P, E, N], U8, name="w_sc", align_bytes=64)
+        nc.vector.memset(w_sc[:].bitcast(I32), 0)
+        for q in range(4):
+            nc.sync.dma_start(
+                out=w_sc[32 * q : 32 * q + 4, :, :].bitcast(I32),
+                in_=w_scales[:, 0, 4 * q : 4 * q + 4, :].bitcast(I32).rearrange("e r n -> r e n"),
+            )
+
+        w_cd = []
+        g_t = []
+
+        def load_weights(half):
+            wt = keep.tile([P, E, 2 * P], I32, name="w_cd%d" % half, align_bytes=64)
+            nc.sync.dma_start(
+                out=wt[:],
+                in_=w_words[:, 0, :, half * 2 * P : (half + 1) * 2 * P, :].rearrange("e p n t -> p e (n t)").bitcast(I32),
+            )
+            w_cd.append(wt)
+
+        def load_gate(b):
+            gt = keep.tile([P, 2, T], F32, name="gate%d" % b)
+            nc.sync.dma_start(out=gt[:], in_=gate[:, b * P : (b + 1) * P, :].rearrange("r p t -> p r t"))
+            g_t.append(gt)
+
+        load_weights(0)
+        nc.sync.dma_start(pos1_t[:], pos1)
+        nc.sync.dma_start(pos2_t[:], pos2)
+        load_gate(0)
+        load_gate(1)
+        load_weights(1)
+        load_gate(2)
+        load_gate(3)
+
+        for i, (raw, t0, cw) in enumerate(x_raw):
+            xg = keep.tile([P, cw, PACK], BF16, name="x_grp%d" % i, align_bytes=64)
+            h = cw // 2
+            nc.vector.tensor_copy(out=xg[:, 0:h, :], in_=raw[:, :, 0:h].rearrange("p j w -> p w j"))
+            nc.scalar.copy(xg[:, h:cw, :], raw[:, :, h:cw].rearrange("p j w -> p w j"))
+            nc.vector.quantize_mx(
+                out=x_codes[:, t0 : t0 + cw].bitcast(FP8X4),
+                scales=x_scales[:, t0 : t0 + cw],
+                in_=xg[:].rearrange("p w j -> p (w j)"),
+            )
+
+        s_codes = keep.tile([P, SLOTS], U32, name="s_codes", align_bytes=64)
+        s_scales = keep.tile([P, SLOTS], U8, name="s_scales", align_bytes=64)
+        y = [keep.tile([P, SLOTS], F32, name="y%d" % b) for b in range(NB)]
+
+        def multiply(b, s0, n_slots, bank):
+            ps = psum.tile([P, n_slots], F32, name="ps_" + bank, tag="ps_" + bank)
+            for e in range(s0 // C, (s0 + n_slots) // C):
+                nc.tensor.matmul_mx(
+                    out=ps[:, e * C - s0 : (e + 1) * C - s0],
+                    lhsT=w_cd[b // 2][:, e, (b % 2) * P : (b % 2 + 1) * P].bitcast(FP8X4),
+                    lhsT_scale=w_sc[:, e, b * P : (b + 1) * P],
+                    rhs=s_codes[:, e * C : (e + 1) * C].bitcast(FP8X4),
+                    rhs_scale=s_scales[:, e * C : (e + 1) * C],
+                    start=True,
+                    stop=True,
+                )
+            return ps
+
+        s0 = 0
+        for n_slots in GATHERS:
+            cols = slice(s0, s0 + n_slots)
+            lst = offs_t[:, s0 // 16 : (s0 + n_slots) // 16]
+            nc.vector.tensor_copy(s_codes[:, cols], x_codes[:].indirect(lst))
+            if s0 + n_slots < SLOTS:
+                nc.vector.tensor_copy(s_scales[:, cols], x_scales[:].indirect(lst))
+            else:
+                for e0 in range(s0, SLOTS, C):
+                    nc.vector.tensor_copy(s_scales[:, e0 : e0 + C], x_scales[:].indirect(offs_t[:, e0 // 16 : (e0 + C) // 16]))
+            s0 += n_slots
+
+        nc.scalar.copy(y[0][:, 0:384], multiply(0, 0, 384, "a")[:])
+        nc.scalar.copy(y[0][:, 384:768], multiply(0, 384, 384, "b")[:])
+        nc.scalar.copy(y[0][:, 768:896], multiply(0, 768, 128, "c")[:])
+        nc.scalar.copy(y[0][:, 896:1024], multiply(0, 896, 128, "d")[:])
+        for b in range(1, NB):
+            nc.scalar.copy(y[b][:, 0:BANK], multiply(b, 0, BANK, "c")[:])
+            nc.scalar.copy(y[b][:, BANK:SLOTS], multiply(b, BANK, BANK, "d")[:])
+
+        first = [keep.tile([P, T], F32, name="first%d" % b) for b in range(NB)]
+        second = [keep.tile([P, T], F32, name="second%d" % b) for b in range(NB)]
+        last = keep.tile([P, T], F32, name="last")
+        summed = keep.tile([P, T + T // 2], F32, name="summed")
+
+        def fetch(dst, b, r, lo, hi):
+            lst = (pos1_t, pos2_t)[r][:, lo // 16 : hi // 16]
+            nc.vector.tensor_tensor(dst[b][:, lo:hi], y[b][:].indirect(lst), g_t[b][:, r, lo:hi], MULT)
+
+        def add_on_vector(dst, b, lo, hi):
+            nc.vector.tensor_tensor(dst[:, lo:hi], first[b][:, lo:hi], second[b][:, lo:hi], ADD)
+            nc.sync.dma_start(out=out[b * P : (b + 1) * P, lo:hi], in_=dst[:, lo:hi])
+
+        def add_on_tensor(dst, b, lo, hi, bank):
+            acc = psum.tile([P, hi - lo], F32, name="ps_" + bank, tag="ps_" + bank)
+            nc.tensor.matmul(acc[:], lhsT=ident[:], rhs=first[b][:, lo:hi], start=True, stop=False)
+            nc.tensor.matmul(acc[:], lhsT=ident[:], rhs=second[b][:, lo:hi], start=False, stop=True)
+            nc.scalar.copy(dst, acc[:])
+            nc.scalar.dma_start(out=out[b * P : (b + 1) * P, lo:hi], in_=dst)
+
+        H = T // 2
+        fetch(first, 0, 0, 0, T)
+        fetch(second, 0, 1, 0, T)
+        add_on_tensor(summed[:, 0:H], 0, 0, H, "c")
+        fetch(first, 1, 0, 0, T)
+        add_on_vector(g_t[1][:, 0, :], 0, H, T)
+        fetch(second, 1, 1, 0, T)
+        add_on_tensor(summed[:, H : H + T], 1, 0, T, "d")
+        fetch(first, 2, 0, 0, T)
+        fetch(second, 2, 1, 0, T)
+        fetch(first, 3, 0, 0, T)
+        add_on_vector(g_t[3][:, 0, :], 2, 0, T)
+        fetch(second, 3, 1, 0, H)
+        fetch(second, 3, 1, H, T)
+        add_on_vector(last, 3, 0, H)
+        add_on_vector(last, 3, H, T)

@@ -131,43 +131,49 @@ def tile_routed_moe_kernel(tc, xT, w_words, w_scales, gate, offs, pos1, pos2, ou
         nc.scalar.copy(y[0][:, 384:768], multiply(0, 384, 384, "b")[:])
         nc.scalar.copy(y[0][:, 768:896], multiply(0, 768, 128, "c")[:])
         nc.scalar.copy(y[0][:, 896:1024], multiply(0, 896, 128, "d")[:])
-        for b in range(1, NB):
-            nc.scalar.copy(y[b][:, 0:BANK], multiply(b, 0, BANK, "c")[:])
-            nc.scalar.copy(y[b][:, BANK:SLOTS], multiply(b, BANK, BANK, "d")[:])
+        for b, banks in ((1, "cd"), (2, "ef"), (3, "gh")):
+            nc.scalar.copy(y[b][:, 0:BANK], multiply(b, 0, BANK, banks[0])[:])
+            nc.scalar.copy(y[b][:, BANK:SLOTS], multiply(b, BANK, BANK, banks[1])[:])
 
         first = [keep.tile([P, T], F32, name="first%d" % b) for b in range(NB)]
         second = [keep.tile([P, T], F32, name="second%d" % b) for b in range(NB)]
         last = keep.tile([P, T], F32, name="last")
-        summed = keep.tile([P, T + T // 2], F32, name="summed")
 
         def fetch(dst, b, r, lo, hi):
             lst = (pos1_t, pos2_t)[r][:, lo // 16 : hi // 16]
             nc.vector.tensor_tensor(dst[b][:, lo:hi], y[b][:].indirect(lst), g_t[b][:, r, lo:hi], MULT)
 
-        def add_on_vector(dst, b, lo, hi):
-            nc.vector.tensor_tensor(dst[:, lo:hi], first[b][:, lo:hi], second[b][:, lo:hi], ADD)
-            nc.sync.dma_start(out=out[b * P : (b + 1) * P, lo:hi], in_=dst[:, lo:hi])
+        def add_on_vector(lo, hi):
+            nc.vector.tensor_tensor(last[:, lo:hi], first[3][:, lo:hi], second[3][:, lo:hi], ADD)
+            nc.sync.dma_start(out=out[3 * P : 4 * P, lo:hi], in_=last[:, lo:hi])
 
-        def add_on_tensor(dst, b, lo, hi, bank):
-            acc = psum.tile([P, hi - lo], F32, name="ps_" + bank, tag="ps_" + bank)
-            nc.tensor.matmul(acc[:], lhsT=ident[:], rhs=first[b][:, lo:hi], start=True, stop=False)
-            nc.tensor.matmul(acc[:], lhsT=ident[:], rhs=second[b][:, lo:hi], start=False, stop=True)
-            nc.scalar.copy(dst, acc[:])
-            nc.scalar.dma_start(out=out[b * P : (b + 1) * P, lo:hi], in_=dst)
+        def add_by_transposes(b, lo, hi, banks):
+            turned = psum.tile([P, hi - lo], F32, name="ps_" + banks[0], tag="ps_" + banks[0])
+            for k in range(lo, hi, P):
+                nc.tensor.matmul(turned[:, k - lo : k - lo + P], lhsT=first[b][:, k : k + P], rhs=ident[:], is_transpose=True, start=True, stop=False)
+                nc.tensor.matmul(turned[:, k - lo : k - lo + P], lhsT=second[b][:, k : k + P], rhs=ident[:], is_transpose=True, start=False, stop=True)
+            turned_sb = keep.tile([P, hi - lo], F32, name="turned_sb%d_%d" % (b, lo))
+            nc.scalar.copy(turned_sb[:], turned[:])
+            back = psum.tile([P, hi - lo], F32, name="ps_" + banks[1], tag="ps_" + banks[1])
+            for k in range(0, hi - lo, P):
+                nc.tensor.transpose(back[:, k : k + P], turned_sb[:, k : k + P], ident[:])
+            summed = keep.tile([P, hi - lo], F32, name="summed%d_%d" % (b, lo))
+            nc.scalar.copy(summed[:], back[:])
+            nc.scalar.dma_start(out=out[b * P : (b + 1) * P, lo:hi], in_=summed[:])
 
         H = T // 2
         fetch(first, 0, 0, 0, T)
         fetch(second, 0, 1, 0, T)
-        add_on_tensor(summed[:, 0:H], 0, 0, H, "c")
+        add_by_transposes(0, 0, T, "gc")
         fetch(first, 1, 0, 0, T)
-        add_on_vector(g_t[1][:, 0, :], 0, H, T)
         fetch(second, 1, 1, 0, T)
-        add_on_tensor(summed[:, H : H + T], 1, 0, T, "d")
+        add_by_transposes(1, 0, T, "hd")
         fetch(first, 2, 0, 0, T)
         fetch(second, 2, 1, 0, T)
+        add_by_transposes(2, 0, H, "ea")
+        add_by_transposes(2, H, T, "fb")
         fetch(first, 3, 0, 0, T)
-        add_on_vector(g_t[3][:, 0, :], 2, 0, T)
         fetch(second, 3, 1, 0, H)
         fetch(second, 3, 1, H, T)
-        add_on_vector(last, 3, 0, H)
-        add_on_vector(last, 3, H, T)
+        add_on_vector(0, H)
+        add_on_vector(H, T)

@@ -143,9 +143,17 @@ def tile_routed_moe_kernel(tc, xT, w_words, w_scales, gate, offs, pos1, pos2, ou
             lst = (pos1_t, pos2_t)[r][:, lo // 16 : hi // 16]
             nc.vector.tensor_tensor(dst[b][:, lo:hi], y[b][:].indirect(lst), g_t[b][:, r, lo:hi], MULT)
 
-        def add_on_vector(lo, hi):
-            nc.vector.tensor_tensor(last[:, lo:hi], first[3][:, lo:hi], second[3][:, lo:hi], ADD)
-            nc.sync.dma_start(out=out[3 * P : 4 * P, lo:hi], in_=last[:, lo:hi])
+        def add_on_vector(dst, b, lo, hi):
+            nc.vector.tensor_tensor(dst[:, lo:hi], first[b][:, lo:hi], second[b][:, lo:hi], ADD)
+            nc.sync.dma_start(out=out[b * P : (b + 1) * P, lo:hi], in_=dst[:, lo:hi])
+
+        def add_on_tensor(b, lo, hi, bank):
+            acc = psum.tile([P, hi - lo], F32, name="ps_" + bank, tag="ps_" + bank)
+            nc.tensor.matmul(acc[:], lhsT=ident[:], rhs=first[b][:, lo:hi], start=True, stop=False)
+            nc.tensor.matmul(acc[:], lhsT=ident[:], rhs=second[b][:, lo:hi], start=False, stop=True)
+            summed = keep.tile([P, hi - lo], F32, name="summed%d_%d" % (b, lo))
+            nc.scalar.copy(summed[:], acc[:])
+            nc.scalar.dma_start(out=out[b * P : (b + 1) * P, lo:hi], in_=summed[:])
 
         def add_by_transposes(b, lo, hi, banks):
             turned = psum.tile([P, hi - lo], F32, name="ps_" + banks[0], tag="ps_" + banks[0])
@@ -167,13 +175,13 @@ def tile_routed_moe_kernel(tc, xT, w_words, w_scales, gate, offs, pos1, pos2, ou
         add_by_transposes(0, 0, T, "gc")
         fetch(first, 1, 0, 0, T)
         fetch(second, 1, 1, 0, T)
-        add_by_transposes(1, 0, T, "hd")
+        add_on_tensor(1, 0, T, "h")
         fetch(first, 2, 0, 0, T)
         fetch(second, 2, 1, 0, T)
-        add_by_transposes(2, 0, H, "ea")
-        add_by_transposes(2, H, T, "fb")
+        add_on_tensor(2, 0, H, "e")
         fetch(first, 3, 0, 0, T)
+        add_on_vector(g_t[3][:, 0, :], 2, H, T)
         fetch(second, 3, 1, 0, H)
         fetch(second, 3, 1, H, T)
-        add_on_vector(0, H)
-        add_on_vector(H, T)
+        add_on_vector(last, 3, 0, H)
+        add_on_vector(last, 3, H, T)

@@ -55,7 +55,8 @@ def tile_routed_moe_kernel(tc, xT, w_words, w_scales, gate, offs, pos1, pos2, ou
 
         w_sc = keep.tile([P, E, N], U8, name="w_sc", align_bytes=64)
         nc.vector.memset(w_sc[:].bitcast(I32), 0)
-        for q in range(4):
+
+        def load_scales(q):
             nc.sync.dma_start(
                 out=w_sc[32 * q : 32 * q + 4, :, :].bitcast(I32),
                 in_=w_scales[:, 0, 4 * q : 4 * q + 4, :].bitcast(I32).rearrange("e r n -> r e n"),
@@ -77,12 +78,16 @@ def tile_routed_moe_kernel(tc, xT, w_words, w_scales, gate, offs, pos1, pos2, ou
             nc.sync.dma_start(out=gt[:], in_=gate[:, b * P : (b + 1) * P, :].rearrange("r p t -> p r t"))
             g_t.append(gt)
 
+        load_scales(0)
+        load_scales(1)
+        load_scales(2)
         load_weights(0)
+        load_scales(3)
         nc.sync.dma_start(pos1_t[:], pos1)
         nc.sync.dma_start(pos2_t[:], pos2)
         load_gate(0)
-        load_gate(1)
         load_weights(1)
+        load_gate(1)
         load_gate(2)
         load_gate(3)
 

@@ -73,9 +73,9 @@ def tile_routed_moe_kernel(tc, xT, w_words, w_scales, gate, offs, pos1, pos2, ou
             )
             w_cd.append(wt)
 
-        def load_gate(b):
-            gt = keep.tile([P, 2, T], F32, name="gate%d" % b)
-            nc.sync.dma_start(out=gt[:], in_=gate[:, b * P : (b + 1) * P, :].rearrange("r p t -> p r t"))
+        def load_gate(b, r):
+            gt = keep.tile([P, T], F32, name="gate%d_%d" % (b, r))
+            nc.sync.dma_start(out=gt[:], in_=gate[r, b * P : (b + 1) * P, :])
             g_t.append(gt)
 
         load_scales(0)
@@ -84,12 +84,16 @@ def tile_routed_moe_kernel(tc, xT, w_words, w_scales, gate, offs, pos1, pos2, ou
         load_weights(0)
         load_scales(3)
         nc.sync.dma_start(pos1_t[:], pos1)
+        load_gate(0, 0)
         nc.sync.dma_start(pos2_t[:], pos2)
-        load_gate(0)
+        load_gate(0, 1)
+        load_gate(1, 0)
         load_weights(1)
-        load_gate(1)
-        load_gate(2)
-        load_gate(3)
+        load_gate(1, 1)
+        load_gate(2, 0)
+        load_gate(2, 1)
+        load_gate(3, 0)
+        load_gate(3, 1)
 
         for i, (raw, t0, cw) in enumerate(x_raw):
             xg = keep.tile([P, cw, PACK], BF16, name="x_grp%d" % i, align_bytes=64)
@@ -146,7 +150,7 @@ def tile_routed_moe_kernel(tc, xT, w_words, w_scales, gate, offs, pos1, pos2, ou
 
         def fetch(dst, b, r, lo, hi):
             lst = (pos1_t, pos2_t)[r][:, lo // 16 : hi // 16]
-            nc.vector.tensor_tensor(dst[b][:, lo:hi], y[b][:].indirect(lst), g_t[b][:, r, lo:hi], MULT)
+            nc.vector.tensor_tensor(dst[b][:, lo:hi], y[b][:].indirect(lst), g_t[2 * b + r][:, lo:hi], MULT)
 
         def add_on_vector(dst, b, lo, hi):
             nc.vector.tensor_tensor(dst[:, lo:hi], first[b][:, lo:hi], second[b][:, lo:hi], ADD)
@@ -185,7 +189,7 @@ def tile_routed_moe_kernel(tc, xT, w_words, w_scales, gate, offs, pos1, pos2, ou
         fetch(second, 2, 1, 0, T)
         add_on_tensor(2, 0, H, "e")
         fetch(first, 3, 0, 0, T)
-        add_on_vector(g_t[3][:, 0, :], 2, H, T)
+        add_on_vector(g_t[6], 2, H, T)
         fetch(second, 3, 1, 0, H)
         fetch(second, 3, 1, H, T)
         add_on_vector(last, 3, 0, H)

@@ -187,9 +187,9 @@ def tile_routed_moe_kernel(tc, xT, w_words, w_scales, gate, offs, pos1, pos2, ou
         add_on_tensor(1, 0, T, "h")
         fetch(first, 2, 0, 0, T)
         fetch(second, 2, 1, 0, T)
+        add_by_transposes(2, H, T, "fa")
         add_on_tensor(2, 0, H, "e")
         fetch(first, 3, 0, 0, T)
-        add_on_vector(g_t[6], 2, H, T)
         fetch(second, 3, 1, 0, H)
         fetch(second, 3, 1, H, T)
         add_on_vector(last, 3, 0, H)

@@ -56,10 +56,10 @@ def tile_routed_moe_kernel(tc, xT, w_words, w_scales, gate, offs, pos1, pos2, ou
         w_sc = keep.tile([P, E, N], U8, name="w_sc", align_bytes=64)
         nc.vector.memset(w_sc[:].bitcast(I32), 0)
 
-        def load_scales(q):
+        def load_scales(r):
             nc.sync.dma_start(
-                out=w_sc[32 * q : 32 * q + 4, :, :].bitcast(I32),
-                in_=w_scales[:, 0, 4 * q : 4 * q + 4, :].bitcast(I32).rearrange("e r n -> r e n"),
+                out=w_sc[r:P:32, :, :].bitcast(I32),
+                in_=w_scales[:, 0, r:16:4, :].bitcast(I32).rearrange("e q n -> q e n"),
             )
 
         w_cd = []

@@ -20,7 +20,9 @@ P = 128
 PACK = 4
 SLOTS = E * C
 NB = N // P
-X_CHUNKS = (256, 128, 128)
+HALF = T // 2
+VECTOR_LOW = 320
+VECTOR_HIGH = 160
 GATHERS = (384, 384, 256)
 BANK = 512
 
@@ -37,13 +39,13 @@ def tile_routed_moe_kernel(tc, xT, w_words, w_scales, gate, offs, pos1, pos2, ou
         pos2_t = lists.tile([P, T // 16], U16, name="pos2_t")
 
         x_view = xT.rearrange("(p j) n -> p j n", j=PACK)
-        x_raw = []
-        t0 = 0
-        for i, cw in enumerate(X_CHUNKS):
-            raw = keep.tile([P, PACK, cw], F32, name="x_raw%d" % i)
-            nc.sync.dma_start(out=raw[:], in_=x_view[:, :, t0 : t0 + cw])
-            x_raw.append((raw, t0, cw))
-            t0 += cw
+        raw_low = keep.tile([P, 2, T], F32, name="raw_low")
+        nc.sync.dma_start(out=raw_low[:], in_=x_view[:, 0:2, :])
+        raw_high = []
+        for h in range(2):
+            raw = keep.tile([P, 2, HALF], F32, name="raw_high%d" % h)
+            nc.sync.dma_start(out=raw[:], in_=x_view[:, 2:4, h * HALF : (h + 1) * HALF])
+            raw_high.append(raw)
         nc.sync.dma_start(offs_t[:], offs)
 
         ident = keep.tile([P, P], F32, name="ident")
@@ -95,15 +97,21 @@ def tile_routed_moe_kernel(tc, xT, w_words, w_scales, gate, offs, pos1, pos2, ou
         load_gate(3, 0)
         load_gate(3, 1)
 
-        for i, (raw, t0, cw) in enumerate(x_raw):
-            xg = keep.tile([P, cw, PACK], BF16, name="x_grp%d" % i, align_bytes=64)
-            h = cw // 2
-            nc.vector.tensor_copy(out=xg[:, 0:h, :], in_=raw[:, :, 0:h].rearrange("p j w -> p w j"))
-            nc.scalar.copy(xg[:, h:cw, :], raw[:, :, h:cw].rearrange("p j w -> p w j"))
+        x_grp = keep.tile([P, T, PACK], BF16, name="x_grp", align_bytes=64)
+
+        def round_rows(j, lo, mid, hi, raw):
+            rows = raw[:].rearrange("p j w -> p w j")
+            nc.vector.tensor_copy(out=x_grp[:, lo:mid, j : j + 2], in_=rows[:, 0 : mid - lo, :])
+            nc.scalar.copy(x_grp[:, mid:hi, j : j + 2], rows[:, mid - lo : hi - lo, :])
+
+        round_rows(0, 0, VECTOR_LOW, T, raw_low)
+        for h in range(2):
+            t0 = h * HALF
+            round_rows(2, t0, t0 + VECTOR_HIGH, t0 + HALF, raw_high[h])
             nc.vector.quantize_mx(
-                out=x_codes[:, t0 : t0 + cw].bitcast(FP8X4),
-                scales=x_scales[:, t0 : t0 + cw],
-                in_=xg[:].rearrange("p w j -> p (w j)"),
+                out=x_codes[:, t0 : t0 + HALF].bitcast(FP8X4),
+                scales=x_scales[:, t0 : t0 + HALF],
+                in_=x_grp[:, t0 : t0 + HALF, :].rearrange("p w j -> p (w j)"),
             )
 
         s_codes = keep.tile([P, SLOTS], U32, name="s_codes", align_bytes=64)

@@ -64,16 +64,17 @@ def tile_routed_moe_kernel(tc, xT, w_words, w_scales, gate, offs, pos1, pos2, ou
                 in_=w_scales[:, 0, r:16:4, :].bitcast(I32).rearrange("e q n -> q e n"),
             )
 
-        w_cd = []
+        w_cd = {}
         g_t = []
 
-        def load_weights(half):
-            wt = keep.tile([P, E, 2 * P], I32, name="w_cd%d" % half, align_bytes=64)
+        def load_weights(half, e0, e1):
+            wt = keep.tile([P, e1 - e0, 2 * P], I32, name="w_cd%d_%d" % (half, e0), align_bytes=64)
             nc.sync.dma_start(
                 out=wt[:],
-                in_=w_words[:, 0, :, half * 2 * P : (half + 1) * 2 * P, :].rearrange("e p n t -> p e (n t)").bitcast(I32),
+                in_=w_words[e0:e1, 0, :, half * 2 * P : (half + 1) * 2 * P, :].rearrange("e p n t -> p e (n t)").bitcast(I32),
             )
-            w_cd.append(wt)
+            for e in range(e0, e1):
+                w_cd[half, e] = wt[:, e - e0, :]
 
         def load_gate(b, r):
             gt = keep.tile([P, T], F32, name="gate%d_%d" % (b, r))
@@ -83,14 +84,15 @@ def tile_routed_moe_kernel(tc, xT, w_words, w_scales, gate, offs, pos1, pos2, ou
         load_scales(0)
         load_scales(1)
         load_scales(2)
-        load_weights(0)
+        load_weights(0, 0, E // 2)
         load_scales(3)
+        load_weights(0, E // 2, E)
         nc.sync.dma_start(pos1_t[:], pos1)
         load_gate(0, 0)
         nc.sync.dma_start(pos2_t[:], pos2)
         load_gate(0, 1)
         load_gate(1, 0)
-        load_weights(1)
+        load_weights(1, 0, E)
         load_gate(1, 1)
         load_gate(2, 0)
         load_gate(2, 1)
@@ -123,7 +125,7 @@ def tile_routed_moe_kernel(tc, xT, w_words, w_scales, gate, offs, pos1, pos2, ou
             for e in range(s0 // C, (s0 + n_slots) // C):
                 nc.tensor.matmul_mx(
                     out=ps[:, e * C - s0 : (e + 1) * C - s0],
-                    lhsT=w_cd[b // 2][:, e, (b % 2) * P : (b % 2 + 1) * P].bitcast(FP8X4),
+                    lhsT=w_cd[b // 2, e][:, (b % 2) * P : (b % 2 + 1) * P].bitcast(FP8X4),
                     lhsT_scale=w_sc[:, e, b * P : (b + 1) * P],
                     rhs=s_codes[:, e * C : (e + 1) * C].bitcast(FP8X4),
                     rhs_scale=s_scales[:, e * C : (e + 1) * C],

from contextlib import ExitStack

import concourse.mybir as mybir
from concourse.masks import make_identity

K, T, E, C, N = 512, 512, 8, 128, 512
FLOPS = 2 * K * N * E * C

F32 = mybir.dt.float32
BF16 = mybir.dt.bfloat16
I32 = mybir.dt.int32
U32 = mybir.dt.uint32
U16 = mybir.dt.uint16
U8 = mybir.dt.uint8
FP8X4 = mybir.dt.float8_e4m3fn_x4
MULT = mybir.AluOpType.mult
ADD = mybir.AluOpType.add

P = 128
PACK = 4
SLOTS = E * C
NB = N // P
HALF = T // 2
VECTOR_LOW = 320
VECTOR_HIGH = 160
GATHERS = (384, 384, 256)
BANK = 512


def tile_routed_moe_kernel(tc, xT, w_words, w_scales, gate, offs, pos1, pos2, out):
    nc = tc.nc
    with ExitStack() as ctx:
        lists = ctx.enter_context(tc.tile_pool(name="lists", bufs=1))
        keep = ctx.enter_context(tc.tile_pool(name="keep", bufs=1))
        psum = ctx.enter_context(tc.psum_pool(name="psum", bufs=1))

        offs_t = lists.tile([P, SLOTS // 16], U16, name="offs_t")
        pos1_t = lists.tile([P, T // 16], U16, name="pos1_t")
        pos2_t = lists.tile([P, T // 16], U16, name="pos2_t")

        x_view = xT.rearrange("(p j) n -> p j n", j=PACK)
        raw_low = keep.tile([P, 2, T], F32, name="raw_low")
        nc.sync.dma_start(out=raw_low[:], in_=x_view[:, 0:2, :])
        raw_high = []
        for h in range(2):
            raw = keep.tile([P, 2, HALF], F32, name="raw_high%d" % h)
            nc.sync.dma_start(out=raw[:], in_=x_view[:, 2:4, h * HALF : (h + 1) * HALF])
            raw_high.append(raw)
        nc.sync.dma_start(offs_t[:], offs)

        ident = keep.tile([P, P], F32, name="ident")
        make_identity(nc, ident[:])

        x_codes = keep.tile([P, T], U32, name="x_codes", align_bytes=64)
        x_scales = keep.tile([P, T], U8, name="x_scales", align_bytes=64)
        nc.gpsimd.memset(x_scales[:], 0)

        w_sc = keep.tile([P, E, N], U8, name="w_sc", align_bytes=64)
        nc.vector.memset(w_sc[:].bitcast(I32), 0)

        def load_scales(r):
            nc.sync.dma_start(
                out=w_sc[r:P:32, :, :].bitcast(I32),
                in_=w_scales[:, 0, r:16:4, :].bitcast(I32).rearrange("e q n -> q e n"),
            )

        w_cd = {}
        g_t = []

        def load_weights(half, e0, e1):
            wt = keep.tile([P, e1 - e0, 2 * P], I32, name="w_cd%d_%d" % (half, e0), align_bytes=64)
            nc.sync.dma_start(
                out=wt[:],
                in_=w_words[e0:e1, 0, :, half * 2 * P : (half + 1) * 2 * P, :].rearrange("e p n t -> p e (n t)").bitcast(I32),
            )
            for e in range(e0, e1):
                w_cd[half, e] = wt[:, e - e0, :]

        def load_gate(b, r):
            gt = keep.tile([P, T], F32, name="gate%d_%d" % (b, r))
            nc.sync.dma_start(out=gt[:], in_=gate[r, b * P : (b + 1) * P, :])
            g_t.append(gt)

        load_scales(0)
        load_scales(1)
        load_scales(2)
        load_weights(0, 0, E // 2)
        load_scales(3)
        load_weights(0, E // 2, E)
        nc.sync.dma_start(pos1_t[:], pos1)
        load_gate(0, 0)
        nc.sync.dma_start(pos2_t[:], pos2)
        load_gate(0, 1)
        load_gate(1, 0)
        load_weights(1, 0, E)
        load_gate(1, 1)
        load_gate(2, 0)
        load_gate(2, 1)
        load_gate(3, 0)
        load_gate(3, 1)

        x_grp = keep.tile([P, T, PACK], BF16, name="x_grp", align_bytes=64)

        def round_rows(j, lo, mid, hi, raw):
            rows = raw[:].rearrange("p j w -> p w j")
            nc.vector.tensor_copy(out=x_grp[:, lo:mid, j : j + 2], in_=rows[:, 0 : mid - lo, :])
            nc.scalar.copy(x_grp[:, mid:hi, j : j + 2], rows[:, mid - lo : hi - lo, :])

        round_rows(0, 0, VECTOR_LOW, T, raw_low)
        for h in range(2):
            t0 = h * HALF
            round_rows(2, t0, t0 + VECTOR_HIGH, t0 + HALF, raw_high[h])
            nc.vector.quantize_mx(
                out=x_codes[:, t0 : t0 + HALF].bitcast(FP8X4),
                scales=x_scales[:, t0 : t0 + HALF],
                in_=x_grp[:, t0 : t0 + HALF, :].rearrange("p w j -> p (w j)"),
            )

        s_codes = keep.tile([P, SLOTS], U32, name="s_codes", align_bytes=64)
        s_scales = keep.tile([P, SLOTS], U8, name="s_scales", align_bytes=64)
        y = [keep.tile([P, SLOTS], F32, name="y%d" % b) for b in range(NB)]

        def multiply(b, s0, n_slots, bank):
            ps = psum.tile([P, n_slots], F32, name="ps_" + bank, tag="ps_" + bank)
            for e in range(s0 // C, (s0 + n_slots) // C):
                nc.tensor.matmul_mx(
                    out=ps[:, e * C - s0 : (e + 1) * C - s0],
                    lhsT=w_cd[b // 2, e][:, (b % 2) * P : (b % 2 + 1) * P].bitcast(FP8X4),
                    lhsT_scale=w_sc[:, e, b * P : (b + 1) * P],
                    rhs=s_codes[:, e * C : (e + 1) * C].bitcast(FP8X4),
                    rhs_scale=s_scales[:, e * C : (e + 1) * C],
                    start=True,
                    stop=True,
                )
            return ps

        s0 = 0
        for n_slots in GATHERS:
            cols = slice(s0, s0 + n_slots)
            lst = offs_t[:, s0 // 16 : (s0 + n_slots) // 16]
            nc.vector.tensor_copy(s_codes[:, cols], x_codes[:].indirect(lst))
            if s0 + n_slots < SLOTS:
                nc.vector.tensor_copy(s_scales[:, cols], x_scales[:].indirect(lst))
            else:
                for e0 in range(s0, SLOTS, C):
                    nc.vector.tensor_copy(s_scales[:, e0 : e0 + C], x_scales[:].indirect(offs_t[:, e0 // 16 : (e0 + C) // 16]))
            s0 += n_slots

        nc.scalar.copy(y[0][:, 0:384], multiply(0, 0, 384, "a")[:])
        nc.scalar.copy(y[0][:, 384:768], multiply(0, 384, 384, "b")[:])
        nc.scalar.copy(y[0][:, 768:896], multiply(0, 768, 128, "c")[:])
        nc.scalar.copy(y[0][:, 896:1024], multiply(0, 896, 128, "d")[:])
        for b, banks in ((1, "cd"), (2, "ef"), (3, "gh")):
            nc.scalar.copy(y[b][:, 0:BANK], multiply(b, 0, BANK, banks[0])[:])
            nc.scalar.copy(y[b][:, BANK:SLOTS], multiply(b, BANK, BANK, banks[1])[:])

        first = [keep.tile([P, T], F32, name="first%d" % b) for b in range(NB)]
        second = [keep.tile([P, T], F32, name="second%d" % b) for b in range(NB)]
        last = keep.tile([P, T], F32, name="last")

        def fetch(dst, b, r, lo, hi):
            lst = (pos1_t, pos2_t)[r][:, lo // 16 : hi // 16]
            nc.vector.tensor_tensor(dst[b][:, lo:hi], y[b][:].indirect(lst), g_t[2 * b + r][:, lo:hi], MULT)

        def add_on_vector(dst, b, lo, hi):
            nc.vector.tensor_tensor(dst[:, lo:hi], first[b][:, lo:hi], second[b][:, lo:hi], ADD)
            nc.sync.dma_start(out=out[b * P : (b + 1) * P, lo:hi], in_=dst[:, lo:hi])

        def add_on_tensor(b, lo, hi, bank):
            acc = psum.tile([P, hi - lo], F32, name="ps_" + bank, tag="ps_" + bank)
            nc.tensor.matmul(acc[:], lhsT=ident[:], rhs=first[b][:, lo:hi], start=True, stop=False)
            nc.tensor.matmul(acc[:], lhsT=ident[:], rhs=second[b][:, lo:hi], start=False, stop=True)
            summed = keep.tile([P, hi - lo], F32, name="summed%d_%d" % (b, lo))
            nc.scalar.copy(summed[:], acc[:])
            nc.scalar.dma_start(out=out[b * P : (b + 1) * P, lo:hi], in_=summed[:])

        def add_by_transposes(b, lo, hi, banks):
            turned = psum.tile([P, hi - lo], F32, name="ps_" + banks[0], tag="ps_" + banks[0])
            for k in range(lo, hi, P):
                nc.tensor.matmul(turned[:, k - lo : k - lo + P], lhsT=first[b][:, k : k + P], rhs=ident[:], is_transpose=True, start=True, stop=False)
                nc.tensor.matmul(turned[:, k - lo : k - lo + P], lhsT=second[b][:, k : k + P], rhs=ident[:], is_transpose=True, start=False, stop=True)
            turned_sb = keep.tile([P, hi - lo], F32, name="turned_sb%d_%d" % (b, lo))
            nc.scalar.copy(turned_sb[:], turned[:])
            back = psum.tile([P, hi - lo], F32, name="ps_" + banks[1], tag="ps_" + banks[1])
            for k in range(0, hi - lo, P):
                nc.tensor.transpose(back[:, k : k + P], turned_sb[:, k : k + P], ident[:])
            summed = keep.tile([P, hi - lo], F32, name="summed%d_%d" % (b, lo))
            nc.scalar.copy(summed[:], back[:])
            nc.scalar.dma_start(out=out[b * P : (b + 1) * P, lo:hi], in_=summed[:])

        H = T // 2
        fetch(first, 0, 0, 0, T)
        fetch(second, 0, 1, 0, T)
        add_by_transposes(0, 0, T, "gc")
        fetch(first, 1, 0, 0, T)
        fetch(second, 1, 1, 0, T)
        add_on_tensor(1, 0, T, "h")
        fetch(first, 2, 0, 0, T)
        fetch(second, 2, 1, 0, T)
        add_by_transposes(2, H, T, "fa")
        add_on_tensor(2, 0, H, "e")
        fetch(first, 3, 0, 0, T)
        fetch(second, 3, 1, 0, H)
        fetch(second, 3, 1, H, T)
        add_on_vector(last, 3, 0, H)
        add_on_vector(last, 3, H, T)
